import numpy as np
import ml_dtypes


def mxq(x, axis, fmt="e4m3"):
    dtype, down = {"e4m3": (ml_dtypes.float8_e4m3fn, 7), "e5m2": (ml_dtypes.float8_e5m2, 14)}[fmt]
    v = np.moveaxis(np.asarray(x, np.float32).astype(ml_dtypes.bfloat16).astype(np.float64), axis, -1)
    blocks = v.reshape(v.shape[:-1] + (-1, 32))
    amax = np.abs(blocks).max(-1, keepdims=True)
    byte = np.maximum(np.where(amax > 0, np.frexp(amax)[1] - 1 + 127, 0) - down, 1)
    scale = np.exp2(byte - 127.0)
    codes = (blocks / scale).astype(np.float32).astype(dtype).astype(np.float64)
    return np.moveaxis((codes * scale).reshape(v.shape), -1, axis)


WIDE = False


def mx_kscale(k):
    if not WIDE:
        return np.ones(k)
    levels = np.array([10, -10, 5, -5, 0])
    if k % 512:
        return np.exp2(np.random.permutation(np.resize(levels, k // 32))).repeat(32)
    a = np.empty((k // 512, 16))
    for p in range(k // 512):
        a[p, :8] = np.random.permutation(np.resize(levels, 8))
        for g in range(8):
            far = levels[np.abs(levels - a[p, g]) >= 10]
            a[p, g + 8] = far[np.random.randint(len(far))]
    return np.exp2(a.ravel()).repeat(32)


def f64(x):
    return np.asarray(x).astype(np.float64)


def striped(idx):
    return np.tile(np.asarray(idx).reshape(-1, 16).T, (8, 1)).astype(np.uint16)


def unstriped(offs):
    return offs[:16].T.reshape(-1).astype(np.int64)


E2M1 = np.array([0.0, 0.5, 1.0, 1.5, 2.0, 3.0, 4.0, 6.0, -0.0, -0.5, -1.0, -1.5, -2.0, -3.0, -4.0, -6.0])


def pack_weight(w, fmt):
    k, n = w.shape
    w = f64(np.asarray(w, np.float32).astype(ml_dtypes.bfloat16)).reshape(k // 32, 32, n)
    amax = np.abs(w).max(1)
    if fmt == "e4m3":
        byte = np.frexp(amax)[1] - 1 + 127 - 7
    else:
        mant, ex = np.frexp(amax / 6.0)
        byte = np.where(mant > 0.5, ex, ex - 1) + 127
    byte = np.clip(np.where(amax > 0, byte, 1), 1, 254)
    scaled = (w * np.exp2(127.0 - byte)[:, None, :]).reshape(k, n).astype(np.float32)
    by_word = np.ascontiguousarray(scaled.reshape(k // 512, 128, 4, n).transpose(0, 1, 3, 2))
    if fmt == "e4m3":
        words = by_word.astype(ml_dtypes.float8_e4m3fn).view(np.uint8)
    else:
        c = by_word.astype(ml_dtypes.float4_e2m1fn).view(np.uint8) & 0xF
        words = (c[..., 0::2] | (c[..., 1::2] << 4)).reshape(k // 512, 128, 2 * n)
    return np.ascontiguousarray(words), np.ascontiguousarray(byte.astype(np.uint8).reshape(k // 512, 16, n))


def unpack_weight(words, scales, fmt):
    g, _, n = scales.shape
    words = np.ascontiguousarray(words).reshape(g, 128, n, -1)
    if fmt == "e4m3":
        vals = words.view(ml_dtypes.float8_e4m3fn).astype(np.float64)
    else:
        nib = np.empty((g, 128, n, 4), np.uint8)
        nib[..., 0::2] = words & 0xF
        nib[..., 1::2] = words >> 4
        vals = E2M1[nib]
    vals = vals * np.repeat(np.exp2(scales.astype(np.float64) - 127.0), 8, axis=1)[..., None]
    return vals.transpose(0, 1, 3, 2).reshape(g * 512, n)


def sigmoid(v):
    return 1.0 / (1.0 + np.exp(-v))


D, K, U, I, E = 512, 512, 1024, 512, 256


def setup_inputs():
    n = np.random.standard_normal
    idx = np.random.permutation(U)[:I]
    idx2 = np.random.permutation(U)[:I]
    idx3 = np.random.permutation(U)[:I]
    fd = mx_kscale(D)
    fk = mx_kscale(K)
    notesp = pack_weight(n((D, U)) / fd[:, None], "e2m1")
    wbp = pack_weight(n((D, K)) * 1.0 / np.sqrt(D) * fd[:, None], "e4m3")
    wop = pack_weight(n((K, E)) * 1.0 / np.sqrt(K) / fk[:, None], "e2m1")
    return {
        "notes_words": notesp[0],
        "notes_scales": notesp[1],
        "wb_words": wbp[0],
        "wb_scales": wbp[1],
        "bias": (np.random.uniform(-0.6, 0.6, (K, 1))).astype(np.float32),
        "slope": (np.random.uniform(0.8, 2.0, (K, 1))).astype(np.float32),
        "kf": (np.random.uniform(0.5, 2.0, (K, 1)) * fk[:, None]).astype(np.float32),
        "wo_words": wop[0],
        "wo_scales": wop[1],
        "offs": striped(idx),
        "offs2": striped(idx2),
        "offs3": striped(idx3),
    }


def reference(notes_words, notes_scales, wb_words, wb_scales, bias, slope, kf, wo_words, wo_scales, offs, offs2, offs3):
    idx = unstriped(offs)
    idx2 = unstriped(offs2)
    idx3 = unstriped(offs3)
    notesu = unpack_weight(notes_words, notes_scales, "e2m1")
    wbu = unpack_weight(wb_words, wb_scales, "e4m3")
    wou = unpack_weight(wo_words, wo_scales, "e2m1")
    h1 = wbu.T @ notesu
    s1 = sigmoid(h1[:, idx] * f64(slope) + f64(bias))
    f1 = np.zeros((K, U))
    f1[:, idx2] = s1
    c1 = h1 + f1 * 2.0
    w = c1[:, idx3] * f64(kf)
    wq = mxq(w, 0, "e4m3")
    y = wou.T @ wq
    return y

@@ -1,0 +1,170 @@
+from contextlib import ExitStack
+
+import concourse.mybir as mybir
+
+D, K, U, I, E = 512, 512, 1024, 512, 256
+FLOPS = 2 * D * K * U + 2 * K * E * I
+
+F32 = mybir.dt.float32
+BF16 = mybir.dt.bfloat16
+I32 = mybir.dt.int32
+U32 = mybir.dt.uint32
+U16 = mybir.dt.uint16
+U8 = mybir.dt.uint8
+FP8X4 = mybir.dt.float8_e4m3fn_x4
+FP4X4 = mybir.dt.float4_e2m1fn_x4
+ACT = mybir.ActivationFunctionType
+ALU = mybir.AluOpType
+
+P = 128
+PACK = 4
+BANK = 512
+HALF = I // 2
+LIST_COLS = I // 16
+
+
+def load_scale_rows(queue, plane, rows, quadrants):
+    for q in quadrants:
+        queue.dma_start(out=plane[32 * q : 32 * q + 4, :].bitcast(I32), in_=rows[4 * q : 4 * q + 4, :].bitcast(I32))
+
+
+def tile_attend_gatehop_kernel(tc, notes_words, notes_scales, wb_words, wb_scales, bias, slope, kf,
+                                wo_words, wo_scales, offs, offs2, offs3, out):
+    nc = tc.nc
+    with ExitStack() as ctx:
+        keep = ctx.enter_context(tc.tile_pool(name="keep", bufs=1))
+        psum = ctx.enter_context(tc.psum_pool(name="psum", bufs=1))
+
+        wb_raw = keep.tile([P, K], U32, tag="early0", align_bytes=64)
+        wb_raw_plane = keep.tile([P, K], U8, tag="early1", align_bytes=64)
+        notes_codes = keep.tile([P, 2 * U], U8, align_bytes=64)
+        notes_plane = keep.tile([P, U], U8, align_bytes=64)
+        wo_codes = keep.tile([P, 2 * E], U8, align_bytes=64)
+        wo_plane = keep.tile([P, E], U8, align_bytes=64)
+        nc.vector.memset(wb_raw_plane[:].bitcast(U32), 0)
+
+        load_scale_rows(nc.sync, notes_plane, notes_scales[0], range(2))
+        load_scale_rows(nc.sync, wb_raw_plane, wb_scales[0], range(1))
+        nc.sync.dma_start(out=wb_raw[:].bitcast(I32), in_=wb_words[0].rearrange("p n t -> p (n t)").bitcast(I32))
+        nc.sync.dma_start(out=notes_codes[:].bitcast(I32), in_=notes_words[0].bitcast(I32))
+        load_scale_rows(nc.sync, wb_raw_plane, wb_scales[0], range(1, 4))
+        load_scale_rows(nc.sync, notes_plane, notes_scales[0], range(2, 4))
+
+        list_h = keep.tile([P, LIST_COLS], U16)
+        list_f = keep.tile([P, LIST_COLS], U16)
+        list_c = keep.tile([P, LIST_COLS], U16)
+        slope_sb = keep.tile([P, PACK], F32)
+        bias_sb = keep.tile([P, PACK], F32)
+        kf_sb = keep.tile([P, PACK], F32)
+        nc.sync.dma_start(list_h[:], offs)
+        nc.gpsimd.dma_start(out=slope_sb[:], in_=slope.rearrange("(p t) o -> p (t o)", t=PACK))
+        nc.gpsimd.dma_start(out=bias_sb[:], in_=bias.rearrange("(p t) o -> p (t o)", t=PACK))
+        nc.sync.dma_start(list_f[:], offs2)
+        nc.sync.dma_start(list_c[:], offs3)
+        nc.sync.dma_start(out=kf_sb[:], in_=kf.rearrange("(p t) o -> p (t o)", t=PACK))
+
+        placed = [keep.tile([P, U], F32, name="placed%d" % t) for t in range(2)]
+        nc.vector.memset(placed[0][:], 0.0)
+        nc.gpsimd.memset(placed[1][:], 0.0)
+        nc.sync.dma_start(out=wo_codes[:].bitcast(I32), in_=wo_words[0].bitcast(I32))
+        load_scale_rows(nc.sync, wo_plane, wo_scales[0], range(4))
+
+        wb_codes = keep.tile([P, K], U32, align_bytes=64)
+        wb_plane = keep.tile([P, K], U8, align_bytes=64)
+        for ts in (slice(0, 1), slice(1, PACK)):
+            for dealt, raw in ((wb_codes, wb_raw), (wb_plane, wb_raw_plane)):
+                nc.vector.tensor_copy(out=dealt[:].rearrange("p (t m) -> p m t", t=PACK)[:, :, ts],
+                                      in_=raw[:].rearrange("p (m t) -> p m t", t=PACK)[:, :, ts])
+        for t in range(2, PACK):
+            placed.append(keep.tile([P, U], F32, name="placed%d" % t, tag="early%d" % (t - 2), align_bytes=64))
+            nc.gpsimd.memset(placed[t][:], 0.0)
+
+        hidden = [keep.tile([P, U], F32, name="hidden%d" % t) for t in range(PACK)]
+        for t in range(PACK):
+            for j in range(U // BANK):
+                acc = psum.tile([P, BANK], F32, name="acc%d_%d" % (t, j), tag="bank%d" % (2 * t + j))
+                nc.tensor.matmul_mx(
+                    out=acc[:],
+                    lhsT=wb_codes[:, t * P : (t + 1) * P].bitcast(FP8X4),
+                    lhsT_scale=wb_plane[:, t * P : (t + 1) * P],
+                    rhs=notes_codes[:, 2 * j * BANK : 2 * (j + 1) * BANK].bitcast(FP4X4),
+                    rhs_scale=notes_plane[:, j * BANK : (j + 1) * BANK],
+                    start=True, stop=True,
+                )
+                nc.vector.tensor_copy(out=hidden[t][:, j * BANK : (j + 1) * BANK], in_=acc[:])
+
+        gate = [keep.tile([P, I], F32, name="gate%d" % t) for t in range(PACK)]
+        for t in range(PACK):
+            nc.scalar.activation(out=gate[t][:], in_=hidden[t][:].indirect(list_h[:]), func=ACT.Sigmoid,
+                                 bias=bias_sb[:, t : t + 1], scale=slope_sb[:, t : t + 1])
+
+        summed = [keep.tile([P, U], F32, name="summed%d" % t) for t in range(PACK)]
+        picked = [keep.tile([P, I], F32, name="picked%d" % t) for t in range(PACK)]
+        pairs = keep.tile([P, 2, I, 2], BF16, align_bytes=64)
+
+        def half_list(offsets, h):
+            return offsets[:, h * LIST_COLS // 2 : (h + 1) * LIST_COLS // 2]
+
+        def scatter_vector(t):
+            nc.vector.tensor_copy(out=placed[t][:].indirect(list_f[:]), in_=gate[t][:])
+
+        def scatter_scalar(t):
+            for h in range(2):
+                nc.scalar.activation(out=placed[t][:].indirect(half_list(list_f, h)),
+                                     in_=gate[t][:, h * HALF : (h + 1) * HALF], func=ACT.Copy)
+
+        def add_up(t):
+            nc.vector.scalar_tensor_tensor(out=summed[t][:], in0=placed[t][:], scalar=2.0, in1=hidden[t][:],
+                                           op0=ALU.mult, op1=ALU.add)
+
+        def pick_scalar(t):
+            nc.scalar.activation(out=picked[t][:], in_=summed[t][:].indirect(list_c[:]), func=ACT.Copy)
+
+        def weigh(t):
+            nc.vector.tensor_scalar(out=pairs[:, t // 2, :, t % 2], in0=picked[t][:], scalar1=kf_sb[:, t : t + 1],
+                                    scalar2=None, op0=ALU.mult)
+
+        scatter_vector(0)
+        scatter_scalar(1)
+        add_up(0)
+        scatter_vector(2)
+        scatter_scalar(3)
+        for t in (1, 2, 3):
+            add_up(t)
+        last = PACK - 1
+        for t in range(last):
+            pick_scalar(t)
+        weigh(0)
+        weigh(1)
+        nc.vector.tensor_copy(out=picked[last][:, :HALF], in_=summed[last][:].indirect(half_list(list_c, 0)))
+        nc.scalar.activation(out=picked[last][:, HALF:], in_=summed[last][:].indirect(half_list(list_c, 1)), func=ACT.Copy)
+        weigh(2)
+        weigh(3)
+        pair_words = pairs[:].rearrange("p u s e -> p (u s e)").bitcast(I32).rearrange("p (u s) -> p u s", u=2)
+        woven = [keep.tile([P, HALF * PACK], BF16, name="woven%d" % h, align_bytes=64) for h in range(2)]
+        for h in range(2):
+            nc.vector.tensor_copy(
+                out=woven[h][:].bitcast(I32).rearrange("p (c i u) -> p c u i", i=4, u=2),
+                in_=pair_words[:, :, h * HALF : (h + 1) * HALF].rearrange("p u (c i) -> p c u i", i=4))
+        for h in range(2):
+            cols = slice(h * HALF, (h + 1) * HALF)
+            w_codes = keep.tile([P, HALF], U32, name="w_codes%d" % h, align_bytes=64)
+            w_plane = keep.tile([P, HALF], U8, name="w_plane%d" % h, align_bytes=64)
+            nc.vector.quantize_mx(out=w_codes[:].bitcast(FP8X4), scales=w_plane[:],
+                                  in_=woven[h][:])
+            for b in range(E // P):
+                acc = psum.tile([P, HALF], F32, name="out_acc%d_%d" % (h, b), tag="bank%d" % (2 * h + b))
+                nc.tensor.matmul_mx(
+                    out=acc[:],
+                    lhsT=wo_codes[:, 2 * b * P : 2 * (b + 1) * P].bitcast(FP4X4),
+                    lhsT_scale=wo_plane[:, b * P : (b + 1) * P],
+                    rhs=w_codes[:].bitcast(FP8X4),
+                    rhs_scale=w_plane[:],
+                    start=True, stop=True,
+                )
+                result = keep.tile([P, HALF], F32, name="result%d_%d" % (h, b))
+                if h == 1 and b == 1:
+                    nc.vector.tensor_copy(out=result[:], in_=acc[:])
+                else:
+                    nc.scalar.copy(out=result[:], in_=acc[:])
+                nc.sync.dma_start(out=out[b * P : (b + 1) * P, cols], in_=result[:])

@@ -35,7 +35,7 @@ def tile_attend_gatehop_kernel(tc, notes_words, notes_scales, wb_words, wb_scale
         keep = ctx.enter_context(tc.tile_pool(name="keep", bufs=1))
         psum = ctx.enter_context(tc.psum_pool(name="psum", bufs=1))
 
-        wb_raw = keep.tile([P, K], U32, tag="early0", align_bytes=64)
+        wb_raw = keep.tile([P, K], U32, align_bytes=64)
         wb_raw_plane = keep.tile([P, K], U8, tag="early1", align_bytes=64)
         notes_codes = keep.tile([P, 2 * U], U8, align_bytes=64)
         notes_plane = keep.tile([P, U], U8, align_bytes=64)
@@ -63,89 +63,122 @@ def tile_attend_gatehop_kernel(tc, notes_words, notes_scales, wb_words, wb_scale
         nc.sync.dma_start(list_c[:], offs3)
         nc.sync.dma_start(out=kf_sb[:], in_=kf.rearrange("(p t) o -> p (t o)", t=PACK))
 
-        placed = [keep.tile([P, U], F32, name="placed%d" % t) for t in range(2)]
+        placed = [keep.tile([P, U], F32, name="placed0")]
         nc.vector.memset(placed[0][:], 0.0)
-        nc.gpsimd.memset(placed[1][:], 0.0)
         nc.sync.dma_start(out=wo_codes[:].bitcast(I32), in_=wo_words[0].bitcast(I32))
         load_scale_rows(nc.sync, wo_plane, wo_scales[0], range(4))
 
-        wb_codes = keep.tile([P, K], U32, align_bytes=64)
-        wb_plane = keep.tile([P, K], U8, align_bytes=64)
-        for ts in (slice(0, 1), slice(1, PACK)):
-            for dealt, raw in ((wb_codes, wb_raw), (wb_plane, wb_raw_plane)):
-                nc.vector.tensor_copy(out=dealt[:].rearrange("p (t m) -> p m t", t=PACK)[:, :, ts],
+        first_codes = keep.tile([P, P], U32, tag="early2", align_bytes=64)
+        first_plane = keep.tile([P, P], U8, tag="early3", align_bytes=64)
+        rest_codes = keep.tile([P, K - P], U32, align_bytes=64)
+        rest_plane = keep.tile([P, K - P], U8, align_bytes=64)
+        for ts, codes, plane in ((slice(0, 1), first_codes, first_plane), (slice(1, PACK), rest_codes, rest_plane)):
+            for dealt, raw in ((codes, wb_raw), (plane, wb_raw_plane)):
+                nc.vector.tensor_copy(out=dealt[:].rearrange("p (t m) -> p m t", m=P),
                                       in_=raw[:].rearrange("p (m t) -> p m t", t=PACK)[:, :, ts])
-        for t in range(2, PACK):
-            placed.append(keep.tile([P, U], F32, name="placed%d" % t, tag="early%d" % (t - 2), align_bytes=64))
-            nc.gpsimd.memset(placed[t][:], 0.0)
+        wb_codes = [first_codes[:]] + [rest_codes[:, t * P : (t + 1) * P] for t in range(PACK - 1)]
+        wb_plane = [first_plane[:]] + [rest_plane[:, t * P : (t + 1) * P] for t in range(PACK - 1)]
+        placed.append(keep.tile([P, U], F32, name="placed1", tag="early1", align_bytes=64))
+        nc.gpsimd.memset(placed[1][:], 0.0)
 
         hidden = [keep.tile([P, U], F32, name="hidden%d" % t) for t in range(PACK)]
+        banks = {}
+        bank_of = {0: (0, 1, 2, 3), 1: (4, 5), 2: (6, 7), 3: (0, 1)}
         for t in range(PACK):
-            for j in range(U // BANK):
-                acc = psum.tile([P, BANK], F32, name="acc%d_%d" % (t, j), tag="bank%d" % (2 * t + j))
+            width = U // len(bank_of[t])
+            for j, bank in enumerate(bank_of[t]):
+                acc = psum.tile([P, width], F32, name="acc%d_%d" % (t, j), tag="bank%d" % bank)
                 nc.tensor.matmul_mx(
                     out=acc[:],
-                    lhsT=wb_codes[:, t * P : (t + 1) * P].bitcast(FP8X4),
-                    lhsT_scale=wb_plane[:, t * P : (t + 1) * P],
-                    rhs=notes_codes[:, 2 * j * BANK : 2 * (j + 1) * BANK].bitcast(FP4X4),
-                    rhs_scale=notes_plane[:, j * BANK : (j + 1) * BANK],
+                    lhsT=wb_codes[t].bitcast(FP8X4),
+                    lhsT_scale=wb_plane[t],
+                    rhs=notes_codes[:, 2 * j * width : 2 * (j + 1) * width].bitcast(FP4X4),
+                    rhs_scale=notes_plane[:, j * width : (j + 1) * width],
                     start=True, stop=True,
                 )
-                nc.vector.tensor_copy(out=hidden[t][:, j * BANK : (j + 1) * BANK], in_=acc[:])
+                nc.vector.tensor_copy(out=hidden[t][:, j * width : (j + 1) * width], in_=acc[:])
+                banks[t, j] = acc
+        for t in range(2, PACK):
+            placed.append(keep.tile([P, U], F32, name="placed%d" % t, tag="early%d" % t, align_bytes=64))
+            nc.gpsimd.memset(placed[t][:], 0.0)
 
-        gate = [keep.tile([P, I], F32, name="gate%d" % t) for t in range(PACK)]
-        for t in range(PACK):
+        gate = [keep.tile([P, I], F32, name="gate%d" % t, tag="gate%d" % t) for t in range(PACK)]
+
+        def fetch_gate(t):
             nc.scalar.activation(out=gate[t][:], in_=hidden[t][:].indirect(list_h[:]), func=ACT.Sigmoid,
                                  bias=bias_sb[:, t : t + 1], scale=slope_sb[:, t : t + 1])
 
-        summed = [keep.tile([P, U], F32, name="summed%d" % t) for t in range(PACK)]
-        picked = [keep.tile([P, I], F32, name="picked%d" % t) for t in range(PACK)]
-        pairs = keep.tile([P, 2, I, 2], BF16, align_bytes=64)
+        summed = [keep.tile([P, U], F32, name="summed%d" % t, tag="summed%d" % t) for t in range(PACK)]
+        picked = [keep.tile([P, I], F32, name="picked%d" % t) for t in range(2)]
+        pairs = keep.tile([P, 2, 2, HALF, 2], BF16, align_bytes=64)
 
         def half_list(offsets, h):
             return offsets[:, h * LIST_COLS // 2 : (h + 1) * LIST_COLS // 2]
 
-        def scatter_vector(t):
-            nc.vector.tensor_copy(out=placed[t][:].indirect(list_f[:]), in_=gate[t][:])
+        def scatter_vector(t, src):
+            nc.vector.tensor_copy(out=placed[t][:].indirect(list_f[:]), in_=src[:])
 
         def scatter_scalar(t):
             for h in range(2):
                 nc.scalar.activation(out=placed[t][:].indirect(half_list(list_f, h)),
-                                     in_=gate[t][:, h * HALF : (h + 1) * HALF], func=ACT.Copy)
+                                     in_=gate[t][:, h * HALF : (h + 1) * HALF], func=ACT.Copy, scale=2.0)
 
-        def add_up(t):
-            nc.vector.scalar_tensor_tensor(out=summed[t][:], in0=placed[t][:], scalar=2.0, in1=hidden[t][:],
-                                           op0=ALU.mult, op1=ALU.add)
+        def add_gpsimd(t):
+            nc.gpsimd.tensor_tensor(out=summed[t][:], in0=placed[t][:], in1=hidden[t][:], op=ALU.add)
+
+        def add_vector(t, factor):
+            for j in range(U // BANK):
+                cols = slice(j * BANK, (j + 1) * BANK)
+                nc.vector.scalar_tensor_tensor(out=summed[t][:, cols], in0=placed[t][:, cols], scalar=factor,
+                                               in1=banks[t, j][:], op0=ALU.mult, op1=ALU.add)
 
         def pick_scalar(t):
             nc.scalar.activation(out=picked[t][:], in_=summed[t][:].indirect(list_c[:]), func=ACT.Copy)
 
-        def weigh(t):
-            nc.vector.tensor_scalar(out=pairs[:, t // 2, :, t % 2], in0=picked[t][:], scalar1=kf_sb[:, t : t + 1],
+        def weigh_vector(t, halves, src):
+            nc.vector.tensor_scalar(out=pairs[:, halves, t // 2, :, t % 2],
+                                    in0=src.rearrange("p (h s) -> p h s", s=HALF), scalar1=kf_sb[:, t : t + 1],
                                     scalar2=None, op0=ALU.mult)
 
-        scatter_vector(0)
+        def weigh_gpsimd(t):
+            nc.gpsimd.tensor_scalar(out=pairs[:, :, t // 2, :, t % 2],
+                                    in0=picked[t][:].rearrange("p (h s) -> p h s", s=HALF), scalar1=kf_sb[:, t : t + 1],
+                                    scalar2=0.0, op0=ALU.mult, op1=ALU.add)
+
+        share = 160
+        fetch_gate(0)
+        fetch_gate(1)
         scatter_scalar(1)
-        add_up(0)
-        scatter_vector(2)
-        scatter_scalar(3)
-        for t in (1, 2, 3):
-            add_up(t)
-        last = PACK - 1
-        for t in range(last):
-            pick_scalar(t)
-        weigh(0)
-        weigh(1)
-        nc.vector.tensor_copy(out=picked[last][:, :HALF], in_=summed[last][:].indirect(half_list(list_c, 0)))
-        nc.scalar.activation(out=picked[last][:, HALF:], in_=summed[last][:].indirect(half_list(list_c, 1)), func=ACT.Copy)
-        weigh(2)
-        weigh(3)
-        pair_words = pairs[:].rearrange("p u s e -> p (u s e)").bitcast(I32).rearrange("p (u s) -> p u s", u=2)
+        fetch_gate(2)
+        fetch_gate(3)
+        nc.vector.tensor_tensor(out=placed[0][:].indirect(list_f[:]), in0=gate[0][:], in1=gate[0][:], op=ALU.add)
+        nc.vector.tensor_copy(out=placed[2][:].indirect(list_f[:, : share // 16]), in_=gate[2][:, :share])
+        nc.scalar.activation(out=placed[2][:].indirect(list_f[:, share // 16 :]), in_=gate[2][:, share:],
+                             func=ACT.Copy)
+        scatter_vector(3, gate[3])
+        add_gpsimd(0)
+        add_gpsimd(1)
+        add_vector(3, 2.0)
+        add_vector(2, 2.0)
+        pick_scalar(0)
+        pick_scalar(1)
+        picked_vector = keep.tile([P, I], F32)
+        nc.vector.tensor_copy(out=picked_vector[:], in_=summed[3][:].indirect(list_c[:]))
+        weigh_gpsimd(0)
+        weigh_gpsimd(1)
+        picked_last = keep.tile([P, I], F32, tag="summed1")
+        for h in range(2):
+            nc.scalar.activation(out=picked_last[:, h * HALF : (h + 1) * HALF],
+                                 in_=summed[2][:].indirect(half_list(list_c, h)), func=ACT.Copy)
+        weigh_vector(3, slice(0, 2), picked_vector[:])
+        for h in range(2):
+            cols = slice(h * HALF, (h + 1) * HALF)
+            weigh_vector(2, slice(h, h + 1), picked_last[:, cols])
         woven = [keep.tile([P, HALF * PACK], BF16, name="woven%d" % h, align_bytes=64) for h in range(2)]
         for h in range(2):
             nc.vector.tensor_copy(
                 out=woven[h][:].bitcast(I32).rearrange("p (c i u) -> p c u i", i=4, u=2),
-                in_=pair_words[:, :, h * HALF : (h + 1) * HALF].rearrange("p u (c i) -> p c u i", i=4))
+                in_=pairs[:, h].rearrange("p u s e -> p (u s e)").bitcast(I32).rearrange("p (u c i) -> p c u i", u=2, i=4))
         for h in range(2):
             cols = slice(h * HALF, (h + 1) * HALF)
             w_codes = keep.tile([P, HALF], U32, name="w_codes%d" % h, align_bytes=64)
@@ -153,7 +186,7 @@ def tile_attend_gatehop_kernel(tc, notes_words, notes_scales, wb_words, wb_scale
             nc.vector.quantize_mx(out=w_codes[:].bitcast(FP8X4), scales=w_plane[:],
                                   in_=woven[h][:])
             for b in range(E // P):
-                acc = psum.tile([P, HALF], F32, name="out_acc%d_%d" % (h, b), tag="bank%d" % (2 * h + b))
+                acc = psum.tile([P, HALF], F32, name="out_acc%d_%d" % (h, b), tag="bank%d" % (2 + 2 * h + b))
                 nc.tensor.matmul_mx(
                     out=acc[:],
                     lhsT=wo_codes[:, 2 * b * P : 2 * (b + 1) * P].bitcast(FP4X4),
@@ -163,7 +196,7 @@ def tile_attend_gatehop_kernel(tc, notes_words, notes_scales, wb_words, wb_scale
                     start=True, stop=True,
                 )
                 result = keep.tile([P, HALF], F32, name="result%d_%d" % (h, b))
-                if h == 1 and b == 1:
+                if b == 1:
                     nc.vector.tensor_copy(out=result[:], in_=acc[:])
                 else:
                     nc.scalar.copy(out=result[:], in_=acc[:])

from contextlib import ExitStack

import concourse.mybir as mybir

D, K, U, I, E = 512, 512, 1024, 512, 256
FLOPS = 2 * D * K * U + 2 * K * E * I

F32 = mybir.dt.float32
BF16 = mybir.dt.bfloat16
I32 = mybir.dt.int32
U32 = mybir.dt.uint32
U16 = mybir.dt.uint16
U8 = mybir.dt.uint8
FP8X4 = mybir.dt.float8_e4m3fn_x4
FP4X4 = mybir.dt.float4_e2m1fn_x4
ACT = mybir.ActivationFunctionType
ALU = mybir.AluOpType

P = 128
PACK = 4
BANK = 512
HALF = I // 2
LIST_COLS = I // 16


def load_scale_rows(queue, plane, rows, quadrants):
    for q in quadrants:
        queue.dma_start(out=plane[32 * q : 32 * q + 4, :].bitcast(I32), in_=rows[4 * q : 4 * q + 4, :].bitcast(I32))


def tile_attend_gatehop_kernel(tc, notes_words, notes_scales, wb_words, wb_scales, bias, slope, kf,
                                wo_words, wo_scales, offs, offs2, offs3, out):
    nc = tc.nc
    with ExitStack() as ctx:
        keep = ctx.enter_context(tc.tile_pool(name="keep", bufs=1))
        psum = ctx.enter_context(tc.psum_pool(name="psum", bufs=1))

        wb_raw = keep.tile([P, K], U32, align_bytes=64)
        wb_raw_plane = keep.tile([P, K], U8, tag="early1", align_bytes=64)
        notes_codes = keep.tile([P, 2 * U], U8, align_bytes=64)
        notes_plane = keep.tile([P, U], U8, align_bytes=64)
        wo_codes = keep.tile([P, 2 * E], U8, align_bytes=64)
        wo_plane = keep.tile([P, E], U8, align_bytes=64)
        nc.vector.memset(wb_raw_plane[:].bitcast(U32), 0)

        load_scale_rows(nc.sync, notes_plane, notes_scales[0], range(2))
        load_scale_rows(nc.sync, wb_raw_plane, wb_scales[0], range(1))
        nc.sync.dma_start(out=wb_raw[:].bitcast(I32), in_=wb_words[0].rearrange("p n t -> p (n t)").bitcast(I32))
        nc.sync.dma_start(out=notes_codes[:].bitcast(I32), in_=notes_words[0].bitcast(I32))
        load_scale_rows(nc.sync, wb_raw_plane, wb_scales[0], range(1, 4))
        load_scale_rows(nc.sync, notes_plane, notes_scales[0], range(2, 4))

        list_h = keep.tile([P, LIST_COLS], U16)
        list_f = keep.tile([P, LIST_COLS], U16)
        list_c = keep.tile([P, LIST_COLS], U16)
        slope_sb = keep.tile([P, PACK], F32)
        bias_sb = keep.tile([P, PACK], F32)
        kf_sb = keep.tile([P, PACK], F32)
        nc.sync.dma_start(list_h[:], offs)
        nc.gpsimd.dma_start(out=slope_sb[:], in_=slope.rearrange("(p t) o -> p (t o)", t=PACK))
        nc.gpsimd.dma_start(out=bias_sb[:], in_=bias.rearrange("(p t) o -> p (t o)", t=PACK))
        nc.sync.dma_start(list_f[:], offs2)
        nc.sync.dma_start(list_c[:], offs3)
        nc.sync.dma_start(out=kf_sb[:], in_=kf.rearrange("(p t) o -> p (t o)", t=PACK))

        placed = [keep.tile([P, U], F32, name="placed0")]
        nc.vector.memset(placed[0][:], 0.0)
        nc.sync.dma_start(out=wo_codes[:].bitcast(I32), in_=wo_words[0].bitcast(I32))
        load_scale_rows(nc.sync, wo_plane, wo_scales[0], range(4))

        first_codes = keep.tile([P, P], U32, tag="early2", align_bytes=64)
        first_plane = keep.tile([P, P], U8, tag="early3", align_bytes=64)
        rest_codes = keep.tile([P, K - P], U32, align_bytes=64)
        rest_plane = keep.tile([P, K - P], U8, align_bytes=64)
        for ts, codes, plane in ((slice(0, 1), first_codes, first_plane), (slice(1, PACK), rest_codes, rest_plane)):
            for dealt, raw in ((codes, wb_raw), (plane, wb_raw_plane)):
                nc.vector.tensor_copy(out=dealt[:].rearrange("p (t m) -> p m t", m=P),
                                      in_=raw[:].rearrange("p (m t) -> p m t", t=PACK)[:, :, ts])
        wb_codes = [first_codes[:]] + [rest_codes[:, t * P : (t + 1) * P] for t in range(PACK - 1)]
        wb_plane = [first_plane[:]] + [rest_plane[:, t * P : (t + 1) * P] for t in range(PACK - 1)]
        placed.append(keep.tile([P, U], F32, name="placed1", tag="early1", align_bytes=64))
        nc.gpsimd.memset(placed[1][:], 0.0)

        hidden = [keep.tile([P, U], F32, name="hidden%d" % t) for t in range(PACK)]
        banks = {}
        bank_of = {0: (0, 1, 2, 3), 1: (4, 5), 2: (6, 7), 3: (0, 1)}
        for t in range(PACK):
            width = U // len(bank_of[t])
            for j, bank in enumerate(bank_of[t]):
                acc = psum.tile([P, width], F32, name="acc%d_%d" % (t, j), tag="bank%d" % bank)
                nc.tensor.matmul_mx(
                    out=acc[:],
                    lhsT=wb_codes[t].bitcast(FP8X4),
                    lhsT_scale=wb_plane[t],
                    rhs=notes_codes[:, 2 * j * width : 2 * (j + 1) * width].bitcast(FP4X4),
                    rhs_scale=notes_plane[:, j * width : (j + 1) * width],
                    start=True, stop=True,
                )
                nc.vector.tensor_copy(out=hidden[t][:, j * width : (j + 1) * width], in_=acc[:])
                banks[t, j] = acc
        for t in range(2, PACK):
            placed.append(keep.tile([P, U], F32, name="placed%d" % t, tag="early%d" % t, align_bytes=64))
            nc.gpsimd.memset(placed[t][:], 0.0)

        gate = [keep.tile([P, I], F32, name="gate%d" % t, tag="gate%d" % t) for t in range(PACK)]

        def fetch_gate(t):
            nc.scalar.activation(out=gate[t][:], in_=hidden[t][:].indirect(list_h[:]), func=ACT.Sigmoid,
                                 bias=bias_sb[:, t : t + 1], scale=slope_sb[:, t : t + 1])

        summed = [keep.tile([P, U], F32, name="summed%d" % t, tag="summed%d" % t) for t in range(PACK)]
        picked = [keep.tile([P, I], F32, name="picked%d" % t) for t in range(2)]
        pairs = keep.tile([P, 2, 2, HALF, 2], BF16, align_bytes=64)

        def half_list(offsets, h):
            return offsets[:, h * LIST_COLS // 2 : (h + 1) * LIST_COLS // 2]

        def scatter_vector(t, src):
            nc.vector.tensor_copy(out=placed[t][:].indirect(list_f[:]), in_=src[:])

        def scatter_scalar(t):
            for h in range(2):
                nc.scalar.activation(out=placed[t][:].indirect(half_list(list_f, h)),
                                     in_=gate[t][:, h * HALF : (h + 1) * HALF], func=ACT.Copy, scale=2.0)

        def add_gpsimd(t):
            nc.gpsimd.tensor_tensor(out=summed[t][:], in0=placed[t][:], in1=hidden[t][:], op=ALU.add)

        def add_vector(t, factor):
            for j in range(U // BANK):
                cols = slice(j * BANK, (j + 1) * BANK)
                nc.vector.scalar_tensor_tensor(out=summed[t][:, cols], in0=placed[t][:, cols], scalar=factor,
                                               in1=banks[t, j][:], op0=ALU.mult, op1=ALU.add)

        def pick_scalar(t):
            nc.scalar.activation(out=picked[t][:], in_=summed[t][:].indirect(list_c[:]), func=ACT.Copy)

        def weigh_vector(t, halves, src):
            nc.vector.tensor_scalar(out=pairs[:, halves, t // 2, :, t % 2],
                                    in0=src.rearrange("p (h s) -> p h s", s=HALF), scalar1=kf_sb[:, t : t + 1],
                                    scalar2=None, op0=ALU.mult)

        def weigh_gpsimd(t):
            nc.gpsimd.tensor_scalar(out=pairs[:, :, t // 2, :, t % 2],
                                    in0=picked[t][:].rearrange("p (h s) -> p h s", s=HALF), scalar1=kf_sb[:, t : t + 1],
                                    scalar2=0.0, op0=ALU.mult, op1=ALU.add)

        share = 160
        fetch_gate(0)
        fetch_gate(1)
        scatter_scalar(1)
        fetch_gate(2)
        fetch_gate(3)
        nc.vector.tensor_tensor(out=placed[0][:].indirect(list_f[:]), in0=gate[0][:], in1=gate[0][:], op=ALU.add)
        nc.vector.tensor_copy(out=placed[2][:].indirect(list_f[:, : share // 16]), in_=gate[2][:, :share])
        nc.scalar.activation(out=placed[2][:].indirect(list_f[:, share // 16 :]), in_=gate[2][:, share:],
                             func=ACT.Copy)
        scatter_vector(3, gate[3])
        add_gpsimd(0)
        add_gpsimd(1)
        add_vector(3, 2.0)
        add_vector(2, 2.0)
        pick_scalar(0)
        pick_scalar(1)
        picked_vector = keep.tile([P, I], F32)
        nc.vector.tensor_copy(out=picked_vector[:], in_=summed[3][:].indirect(list_c[:]))
        weigh_gpsimd(0)
        weigh_gpsimd(1)
        picked_last = keep.tile([P, I], F32, tag="summed1")
        for h in range(2):
            nc.scalar.activation(out=picked_last[:, h * HALF : (h + 1) * HALF],
                                 in_=summed[2][:].indirect(half_list(list_c, h)), func=ACT.Copy)
        weigh_vector(3, slice(0, 2), picked_vector[:])
        for h in range(2):
            cols = slice(h * HALF, (h + 1) * HALF)
            weigh_vector(2, slice(h, h + 1), picked_last[:, cols])
        woven = [keep.tile([P, HALF * PACK], BF16, name="woven%d" % h, align_bytes=64) for h in range(2)]
        for h in range(2):
            nc.vector.tensor_copy(
                out=woven[h][:].bitcast(I32).rearrange("p (c i u) -> p c u i", i=4, u=2),
                in_=pairs[:, h].rearrange("p u s e -> p (u s e)").bitcast(I32).rearrange("p (u c i) -> p c u i", u=2, i=4))
        for h in range(2):
            cols = slice(h * HALF, (h + 1) * HALF)
            w_codes = keep.tile([P, HALF], U32, name="w_codes%d" % h, align_bytes=64)
            w_plane = keep.tile([P, HALF], U8, name="w_plane%d" % h, align_bytes=64)
            nc.vector.quantize_mx(out=w_codes[:].bitcast(FP8X4), scales=w_plane[:],
                                  in_=woven[h][:])
            for b in range(E // P):
                acc = psum.tile([P, HALF], F32, name="out_acc%d_%d" % (h, b), tag="bank%d" % (2 + 2 * h + b))
                nc.tensor.matmul_mx(
                    out=acc[:],
                    lhsT=wo_codes[:, 2 * b * P : 2 * (b + 1) * P].bitcast(FP4X4),
                    lhsT_scale=wo_plane[:, b * P : (b + 1) * P],
                    rhs=w_codes[:].bitcast(FP8X4),
                    rhs_scale=w_plane[:],
                    start=True, stop=True,
                )
                result = keep.tile([P, HALF], F32, name="result%d_%d" % (h, b))
                if b == 1:
                    nc.vector.tensor_copy(out=result[:], in_=acc[:])
                else:
                    nc.scalar.copy(out=result[:], in_=acc[:])
                nc.sync.dma_start(out=out[b * P : (b + 1) * P, cols], in_=result[:])
